import numpy as np
CORES = [0,4,8,12,16,20,24,28]
N = 8
ROOT = 5
def setup_inputs(rng):
    return {"x": rng.standard_normal((N, 128, 1024), dtype=np.float32)}
def reference(x):
    y = np.full(x.shape, np.nan, x.dtype)
    y[ROOT] = x.sum(axis=0, dtype=np.float64).astype(x.dtype)
    return {"y": y}

@@ -1,0 +1,106 @@
+from concourse.bass import DstId, RemoteDMATransfer
+from concourse.mybir import AluOpType
+
+CH = [32, 32, 32, 32]
+C = len(CH)
+FOLD = (2, 3, 6, 7)
+ROOT = 20
+ORDER = [("z", 0), ("z", 1), ("z", 2), ("t", 0), ("z", 3), ("t", 1), ("t", 2), ("t", 3)]
+
+
+def _n(c):
+    return CH[c] * 2
+
+
+SCRATCH = {
+    "s16": ("dram", [2, 128, 512], "float32"),
+    "l16": ("dram", [2, 128, 512], "float32"),
+}
+SEMAPHORES = ["sent", "cp", "a16", "q16", "q3"]
+for _c in range(C):
+    SCRATCH["st%d" % _c] = ("dram", [4, 128, _n(_c)], "float32")
+    SCRATCH["la%d" % _c] = ("dram", [128, _n(_c)], "float32")
+    SCRATCH["lb%d" % _c] = ("dram", [128, _n(_c)], "float32")
+    SCRATCH["lp%d" % _c] = ("dram", [128, _n(_c)], "float32")
+    SCRATCH["rz%d" % _c] = ("dram", [4, 128, _n(_c)], "float32")
+    SCRATCH["rt%d" % _c] = ("dram", [4, 128, _n(_c)], "float32")
+    SEMAPHORES += ["ld%d" % _c, "in%d" % _c, "z%d" % _c, "t%d" % _c, "qz%d" % _c]
+
+
+def _dst(topo, core):
+    a = topo.addr(core)
+    return DstId(rid=a[0], pnc=a[1])
+
+
+def rank_program(g, core, T, topo):
+    chip, k = core // 8, core % 8
+    start = [sum(CH[:c]) for c in range(C)]
+
+    if core == ROOT:
+        g.sync.dma_start(T.y[0:64, :], T.x[0:64, :]).then_inc(T.sem.cp, 16)
+        g.scalar.dma_start(T.y[64:128, :], T.x[64:128, :]).then_inc(T.sem.cp, 16)
+        g.wait_ge(T.sem.cp, 32)
+        g.wait_ge(T.sem.a16, 32)
+        g.dma_start(T.y[:, :], T.l16[:], accum_op=AluOpType.add, max_dma_last_dim=8192).then_inc(T.sem.q16, 16)
+        g.wait_ge(T.sem.q16, 16)
+        for kind, c in ORDER:
+            rows = T.y[start[c]:start[c] + CH[c], :]
+            g.wait_ge(T.sem["%s%d" % (kind, c)], 32)
+            if kind == "z":
+                g.dma_start(rows, T["rz%d" % c][:], accum_op=AluOpType.add,
+                            max_dma_last_dim=8192).then_inc(T.sem["qz%d" % c], 16)
+            else:
+                g.wait_ge(T.sem["qz%d" % c], 16)
+                g.dma_start(rows, T["rt%d" % c][:], accum_op=AluOpType.add,
+                            max_dma_last_dim=8192).then_inc(T.sem.q3, 16)
+        g.wait_ge(T.sem.q3, 16 * C)
+        return
+
+    if core == 16:
+        a = topo.addr(ROOT)
+        for i, q in enumerate((g.sync, g.scalar)):
+            q.dma_start(T.s16[i], T.x[64 * i:64 * i + 64, :]).then_inc(T.sem["ld%d" % i], 16)
+        for i in range(2):
+            g.wait_ge(T.sem["ld%d" % i], 16)
+            g.remote_dma(T.l16[i], T.s16[i], T.sem.a16, T.sem.sent, a[1], a[0], 0xFFFF)
+        g.wait_ge(T.sem.sent, 32)
+        return
+
+    if chip == 2:
+        return
+
+    if k in (0, 4):
+        land = "la" if k == 0 else "lb"
+        for c in range(C):
+            q = g.sync if c % 2 == 0 else g.scalar
+            q.dma_start(T["st%d" % c][:], T.x[start[c]:start[c] + CH[c], :]).then_inc(T.sem["ld%d" % c], 16)
+        for c in range(C):
+            g.wait_ge(T.sem["ld%d" % c], 16)
+            g.remote_dma_fused(
+                [RemoteDMATransfer(dst_ids=[_dst(topo, chip * 8 + FOLD[h])], dma_engine_mask=0xF << (4 * h),
+                                   remote_sem=T.sem["in%d" % c], src=T["st%d" % c][h],
+                                   dst=T["%s%d" % (land, c)][:]) for h in range(4)],
+                local_sem=T.sem.sent)
+        g.wait_ge(T.sem.sent, 16 * C)
+        return
+
+    if k in FOLD:
+        h = FOLD.index(k)
+        for c in range(C):
+            srcs = [T["la%d" % c][:], T["lb%d" % c][:]]
+            need = 8
+            if chip == 3:
+                srcs.append(T["lp%d" % c][:])
+                need += 8
+            if chip == 1:
+                to, out, sem = 24 + k, T["lp%d" % c][:], T.sem["in%d" % c]
+            elif chip == 0:
+                to, out, sem = ROOT, T["rz%d" % c][h], T.sem["z%d" % c]
+            else:
+                to, out, sem = ROOT, T["rt%d" % c][h], T.sem["t%d" % c]
+            g.wait_ge(T.sem["in%d" % c], need)
+            g.remote_dma_fused(
+                [RemoteDMATransfer(dst_ids=[_dst(topo, to)], dma_engine_mask=0x00FF, remote_sem=sem,
+                                   srcs=srcs, dsts=[out], alu_op=1)],
+                local_sem=T.sem.sent)
+        g.wait_ge(T.sem.sent, 8 * C)

@@ -1,30 +1,28 @@
 from concourse.bass import DstId, RemoteDMATransfer
 from concourse.mybir import AluOpType
 
-CH = [32, 32, 32, 32]
-C = len(CH)
+S = 2
+BR = 128 // S
+CR = BR // 2
+N = CR * 2
 FOLD = (2, 3, 6, 7)
 ROOT = 20
-ORDER = [("z", 0), ("z", 1), ("z", 2), ("t", 0), ("z", 3), ("t", 1), ("t", 2), ("t", 3)]
-
-
-def _n(c):
-    return CH[c] * 2
-
+LATE = {0: 1, 3: 0}
 
 SCRATCH = {
     "s16": ("dram", [2, 128, 512], "float32"),
     "l16": ("dram", [2, 128, 512], "float32"),
+    "st": ("dram", [8 * S, 128, N], "float32"),
+    "la": ("dram", [2 * S, 128, N], "float32"),
+    "lb": ("dram", [2 * S, 128, N], "float32"),
+    "lp": ("dram", [S, 128, N], "float32"),
+    "rearly": ("dram", [8 * S, 128, N], "float32"),
+    "rlate": ("dram", [8 * S, 128, N], "float32"),
 }
-SEMAPHORES = ["sent", "cp", "a16", "q16", "q3"]
-for _c in range(C):
-    SCRATCH["st%d" % _c] = ("dram", [4, 128, _n(_c)], "float32")
-    SCRATCH["la%d" % _c] = ("dram", [128, _n(_c)], "float32")
-    SCRATCH["lb%d" % _c] = ("dram", [128, _n(_c)], "float32")
-    SCRATCH["lp%d" % _c] = ("dram", [128, _n(_c)], "float32")
-    SCRATCH["rz%d" % _c] = ("dram", [4, 128, _n(_c)], "float32")
-    SCRATCH["rt%d" % _c] = ("dram", [4, 128, _n(_c)], "float32")
-    SEMAPHORES += ["ld%d" % _c, "in%d" % _c, "z%d" % _c, "t%d" % _c, "qz%d" % _c]
+SEMAPHORES = ["sent", "cp", "a0", "a1", "q0", "q1", "ql"]
+for _s in range(S):
+    SEMAPHORES += ["ld%d" % (2 * _s), "ld%d" % (2 * _s + 1), "in%d" % (2 * _s), "in%d" % (2 * _s + 1),
+                   "e%d" % _s, "l%d" % _s, "qe%d" % _s]
 
 
 def _dst(topo, core):
@@ -34,26 +32,28 @@ def _dst(topo, core):
 
 def rank_program(g, core, T, topo):
     chip, k = core // 8, core % 8
-    start = [sum(CH[:c]) for c in range(C)]
+    add = AluOpType.add
 
     if core == ROOT:
         g.sync.dma_start(T.y[0:64, :], T.x[0:64, :]).then_inc(T.sem.cp, 16)
         g.scalar.dma_start(T.y[64:128, :], T.x[64:128, :]).then_inc(T.sem.cp, 16)
         g.wait_ge(T.sem.cp, 32)
-        g.wait_ge(T.sem.a16, 32)
-        g.dma_start(T.y[:, :], T.l16[:], accum_op=AluOpType.add, max_dma_last_dim=8192).then_inc(T.sem.q16, 16)
-        g.wait_ge(T.sem.q16, 16)
-        for kind, c in ORDER:
-            rows = T.y[start[c]:start[c] + CH[c], :]
-            g.wait_ge(T.sem["%s%d" % (kind, c)], 32)
-            if kind == "z":
-                g.dma_start(rows, T["rz%d" % c][:], accum_op=AluOpType.add,
-                            max_dma_last_dim=8192).then_inc(T.sem["qz%d" % c], 16)
-            else:
-                g.wait_ge(T.sem["qz%d" % c], 16)
-                g.dma_start(rows, T["rt%d" % c][:], accum_op=AluOpType.add,
-                            max_dma_last_dim=8192).then_inc(T.sem.q3, 16)
-        g.wait_ge(T.sem.q3, 16 * C)
+        for i in range(2):
+            g.wait_ge(T.sem["a%d" % i], 16)
+            g.dma_start(T.y[64 * i:64 * i + 64, :], T.l16[i], accum_op=add,
+                        max_dma_last_dim=8192).then_inc(T.sem["q%d" % i], 16)
+        for s in range(S):
+            g.wait_ge(T.sem["e%d" % s], 64)
+            if s % (S // 2) == 0:
+                g.wait_ge(T.sem["q%d" % (2 * s // S)], 16)
+            g.dma_start(T.y[BR * s:BR * s + BR, :], T.rearly[8 * s:8 * s + 8], accum_op=add,
+                        max_dma_last_dim=8192).then_inc(T.sem["qe%d" % s], 16)
+        for s in range(S):
+            g.wait_ge(T.sem["l%d" % s], 64)
+            g.wait_ge(T.sem["qe%d" % s], 16)
+            g.dma_start(T.y[BR * s:BR * s + BR, :], T.rlate[8 * s:8 * s + 8], accum_op=add,
+                        max_dma_last_dim=8192).then_inc(T.sem.ql, 16)
+        g.wait_ge(T.sem.ql, 16 * S)
         return
 
     if core == 16:
@@ -62,45 +62,72 @@ def rank_program(g, core, T, topo):
             q.dma_start(T.s16[i], T.x[64 * i:64 * i + 64, :]).then_inc(T.sem["ld%d" % i], 16)
         for i in range(2):
             g.wait_ge(T.sem["ld%d" % i], 16)
-            g.remote_dma(T.l16[i], T.s16[i], T.sem.a16, T.sem.sent, a[1], a[0], 0xFFFF)
+            g.remote_dma(T.l16[i], T.s16[i], T.sem["a%d" % i], T.sem.sent, a[1], a[0], 0xFFFF)
         g.wait_ge(T.sem.sent, 32)
         return
 
     if chip == 2:
         return
 
+    land = T.la if k == 0 else T.lb
+
+    if k in (0, 4) and chip == 1:
+        for s in range(S):
+            q = g.sync if s % 2 == 0 else g.scalar
+            q.dma_start(T.st[8 * s:8 * s + 8], T.x[BR * s:BR * s + BR, :]).then_inc(T.sem["ld%d" % s], 16)
+        for s in range(S):
+            g.wait_ge(T.sem["ld%d" % s], 16)
+            g.remote_dma_fused(
+                [RemoteDMATransfer(dst_ids=[_dst(topo, chip * 8 + FOLD[h])], dma_engine_mask=0x3 << (8 * r + 2 * h),
+                                   remote_sem=T.sem["in%d" % s], src=T.st[8 * s + 4 * r + h],
+                                   dst=land[2 * s + r]) for r in range(2) for h in range(4)],
+                local_sem=T.sem.sent)
+        g.wait_ge(T.sem.sent, 16 * S)
+        return
+
     if k in (0, 4):
-        land = "la" if k == 0 else "lb"
-        for c in range(C):
-            q = g.sync if c % 2 == 0 else g.scalar
-            q.dma_start(T["st%d" % c][:], T.x[start[c]:start[c] + CH[c], :]).then_inc(T.sem["ld%d" % c], 16)
-        for c in range(C):
+        late = LATE[chip]
+        order = [2 * s + (1 - late) for s in range(S)] + [2 * s + late for s in range(S)]
+        for i, c in enumerate(order):
+            q = g.sync if i % 2 == 0 else g.scalar
+            q.dma_start(T.st[4 * c:4 * c + 4], T.x[CR * c:CR * c + CR, :]).then_inc(T.sem["ld%d" % c], 16)
+        for c in order:
             g.wait_ge(T.sem["ld%d" % c], 16)
             g.remote_dma_fused(
                 [RemoteDMATransfer(dst_ids=[_dst(topo, chip * 8 + FOLD[h])], dma_engine_mask=0xF << (4 * h),
-                                   remote_sem=T.sem["in%d" % c], src=T["st%d" % c][h],
-                                   dst=T["%s%d" % (land, c)][:]) for h in range(4)],
+                                   remote_sem=T.sem["in%d" % c], src=T.st[4 * c + h],
+                                   dst=land[c]) for h in range(4)],
                 local_sem=T.sem.sent)
-        g.wait_ge(T.sem.sent, 16 * C)
+        g.wait_ge(T.sem.sent, 32 * S)
+        return
+
+    if k in FOLD and chip == 1:
+        for s in range(S):
+            g.wait_ge(T.sem["in%d" % s], 8)
+            g.remote_dma_fused(
+                [RemoteDMATransfer(dst_ids=[_dst(topo, (3, 0)[r] * 8 + k)], dma_engine_mask=0xF << (4 * r),
+                                   remote_sem=T.sem["in%d" % (2 * s + r)],
+                                   srcs=[T.la[2 * s + r], T.lb[2 * s + r]], dsts=[T.lp[s]], alu_op=1)
+                 for r in range(2)],
+                local_sem=T.sem.sent)
+        g.wait_ge(T.sem.sent, 8 * S)
         return
 
     if k in FOLD:
         h = FOLD.index(k)
-        for c in range(C):
-            srcs = [T["la%d" % c][:], T["lb%d" % c][:]]
-            need = 8
-            if chip == 3:
-                srcs.append(T["lp%d" % c][:])
-                need += 8
-            if chip == 1:
-                to, out, sem = 24 + k, T["lp%d" % c][:], T.sem["in%d" % c]
-            elif chip == 0:
-                to, out, sem = ROOT, T["rz%d" % c][h], T.sem["z%d" % c]
-            else:
-                to, out, sem = ROOT, T["rt%d" % c][h], T.sem["t%d" % c]
-            g.wait_ge(T.sem["in%d" % c], need)
-            g.remote_dma_fused(
-                [RemoteDMATransfer(dst_ids=[_dst(topo, to)], dma_engine_mask=0x00FF, remote_sem=sem,
-                                   srcs=srcs, dsts=[out], alu_op=1)],
-                local_sem=T.sem.sent)
-        g.wait_ge(T.sem.sent, 8 * C)
+        late = LATE[chip]
+        for r in (1 - late, late):
+            for s in range(S):
+                c = 2 * s + r
+                srcs = [T.la[c], T.lb[c]]
+                need = 8
+                if r == late:
+                    srcs.append(T.lp[s])
+                    need += 4
+                g.wait_ge(T.sem["in%d" % c], need)
+                g.remote_dma_fused(
+                    [RemoteDMATransfer(dst_ids=[_dst(topo, ROOT)], dma_engine_mask=0x00FF,
+                                       remote_sem=T.sem[("l%d" if r == late else "e%d") % s],
+                                       srcs=srcs, dsts=[(T.rlate if r == late else T.rearly)[4 * c + h]], alu_op=1)],
+                    local_sem=T.sem.sent)
+        g.wait_ge(T.sem.sent, 16 * S)

@@ -1,5 +1,4 @@
 from concourse.bass import DstId, RemoteDMATransfer
-from concourse.mybir import AluOpType
 
 S = 2
 BR = 128 // S
@@ -7,22 +6,21 @@ CR = BR // 2
 N = CR * 2
 FOLD = (2, 3, 6, 7)
 ROOT = 20
-LATE = {0: 1, 3: 0}
+MINE = {0: 1, 3: 0}
+GATHER = (3, 0)
 
 SCRATCH = {
-    "s16": ("dram", [2, 128, 512], "float32"),
-    "l16": ("dram", [2, 128, 512], "float32"),
     "st": ("dram", [8 * S, 128, N], "float32"),
     "la": ("dram", [2 * S, 128, N], "float32"),
     "lb": ("dram", [2 * S, 128, N], "float32"),
     "lp": ("dram", [S, 128, N], "float32"),
-    "rearly": ("dram", [8 * S, 128, N], "float32"),
-    "rlate": ("dram", [8 * S, 128, N], "float32"),
+    "lr": ("dram", [S, 128, N], "float32"),
+    "lq": ("dram", [S, 128, N], "float32"),
+    "rsum": ("dram", [8 * S, 128, N], "float32"),
 }
-SEMAPHORES = ["sent", "cp", "a0", "a1", "q0", "q1", "ql"]
+SEMAPHORES = ["sent", "fin"]
 for _s in range(S):
-    SEMAPHORES += ["ld%d" % (2 * _s), "ld%d" % (2 * _s + 1), "in%d" % (2 * _s), "in%d" % (2 * _s + 1),
-                   "e%d" % _s, "l%d" % _s, "qe%d" % _s]
+    SEMAPHORES += ["ld%d" % (2 * _s), "ld%d" % (2 * _s + 1), "in%d" % (2 * _s), "in%d" % (2 * _s + 1), "l%d" % _s]
 
 
 def _dst(topo, core):
@@ -32,49 +30,13 @@ def _dst(topo, core):
 
 def rank_program(g, core, T, topo):
     chip, k = core // 8, core % 8
-    add = AluOpType.add
-
-    if core == ROOT:
-        g.sync.dma_start(T.y[0:64, :], T.x[0:64, :]).then_inc(T.sem.cp, 16)
-        g.scalar.dma_start(T.y[64:128, :], T.x[64:128, :]).then_inc(T.sem.cp, 16)
-        g.wait_ge(T.sem.cp, 32)
-        for i in range(2):
-            g.wait_ge(T.sem["a%d" % i], 16)
-            g.dma_start(T.y[64 * i:64 * i + 64, :], T.l16[i], accum_op=add,
-                        max_dma_last_dim=8192).then_inc(T.sem["q%d" % i], 16)
-        for s in range(S):
-            g.wait_ge(T.sem["e%d" % s], 64)
-            if s % (S // 2) == 0:
-                g.wait_ge(T.sem["q%d" % (2 * s // S)], 16)
-            g.dma_start(T.y[BR * s:BR * s + BR, :], T.rearly[8 * s:8 * s + 8], accum_op=add,
-                        max_dma_last_dim=8192).then_inc(T.sem["qe%d" % s], 16)
-        for s in range(S):
-            g.wait_ge(T.sem["l%d" % s], 64)
-            g.wait_ge(T.sem["qe%d" % s], 16)
-            g.dma_start(T.y[BR * s:BR * s + BR, :], T.rlate[8 * s:8 * s + 8], accum_op=add,
-                        max_dma_last_dim=8192).then_inc(T.sem.ql, 16)
-        g.wait_ge(T.sem.ql, 16 * S)
-        return
-
-    if core == 16:
-        a = topo.addr(ROOT)
-        for i, q in enumerate((g.sync, g.scalar)):
-            q.dma_start(T.s16[i], T.x[64 * i:64 * i + 64, :]).then_inc(T.sem["ld%d" % i], 16)
-        for i in range(2):
-            g.wait_ge(T.sem["ld%d" % i], 16)
-            g.remote_dma(T.l16[i], T.s16[i], T.sem["a%d" % i], T.sem.sent, a[1], a[0], 0xFFFF)
-        g.wait_ge(T.sem.sent, 32)
-        return
-
-    if chip == 2:
-        return
-
     land = T.la if k == 0 else T.lb
+    queues = (g.sync, g.scalar)
 
-    if k in (0, 4) and chip == 1:
+    if k in (0, 4) and chip in (1, 2):
         for s in range(S):
-            q = g.sync if s % 2 == 0 else g.scalar
-            q.dma_start(T.st[8 * s:8 * s + 8], T.x[BR * s:BR * s + BR, :]).then_inc(T.sem["ld%d" % s], 16)
+            queues[s % 2].dma_start(T.st[8 * s:8 * s + 8],
+                                    T.x[BR * s:BR * s + BR, :]).then_inc(T.sem["ld%d" % s], 16)
         for s in range(S):
             g.wait_ge(T.sem["ld%d" % s], 16)
             g.remote_dma_fused(
@@ -82,15 +44,21 @@ def rank_program(g, core, T, topo):
                                    remote_sem=T.sem["in%d" % s], src=T.st[8 * s + 4 * r + h],
                                    dst=land[2 * s + r]) for r in range(2) for h in range(4)],
                 local_sem=T.sem.sent)
+        if core == ROOT:
+            for s in range(S):
+                queues[s % 2].wait_ge(T.sem["l%d" % s], 64)
+                queues[s % 2].dma_start(T.y[BR * s:BR * s + BR, :], T.rsum[8 * s:8 * s + 8]).then_inc(T.sem.fin, 16)
         g.wait_ge(T.sem.sent, 16 * S)
+        if core == ROOT:
+            g.wait_ge(T.sem.fin, 16 * S)
         return
 
     if k in (0, 4):
-        late = LATE[chip]
-        order = [2 * s + (1 - late) for s in range(S)] + [2 * s + late for s in range(S)]
+        mine = MINE[chip]
+        order = [2 * s + (1 - mine) for s in range(S)] + [2 * s + mine for s in range(S)]
         for i, c in enumerate(order):
-            q = g.sync if i % 2 == 0 else g.scalar
-            q.dma_start(T.st[4 * c:4 * c + 4], T.x[CR * c:CR * c + CR, :]).then_inc(T.sem["ld%d" % c], 16)
+            queues[i % 2].dma_start(T.st[4 * c:4 * c + 4],
+                                    T.x[CR * c:CR * c + CR, :]).then_inc(T.sem["ld%d" % c], 16)
         for c in order:
             g.wait_ge(T.sem["ld%d" % c], 16)
             g.remote_dma_fused(
@@ -101,13 +69,14 @@ def rank_program(g, core, T, topo):
         g.wait_ge(T.sem.sent, 32 * S)
         return
 
-    if k in FOLD and chip == 1:
+    if k in FOLD and chip in (1, 2):
+        out = T.lp if chip == 1 else T.lr
         for s in range(S):
             g.wait_ge(T.sem["in%d" % s], 8)
             g.remote_dma_fused(
-                [RemoteDMATransfer(dst_ids=[_dst(topo, (3, 0)[r] * 8 + k)], dma_engine_mask=0xF << (4 * r),
+                [RemoteDMATransfer(dst_ids=[_dst(topo, GATHER[r] * 8 + k)], dma_engine_mask=0xF << (4 * r),
                                    remote_sem=T.sem["in%d" % (2 * s + r)],
-                                   srcs=[T.la[2 * s + r], T.lb[2 * s + r]], dsts=[T.lp[s]], alu_op=1)
+                                   srcs=[T.la[2 * s + r], T.lb[2 * s + r]], dsts=[out[s]], alu_op=1)
                  for r in range(2)],
                 local_sem=T.sem.sent)
         g.wait_ge(T.sem.sent, 8 * S)
@@ -115,19 +84,22 @@ def rank_program(g, core, T, topo):
 
     if k in FOLD:
         h = FOLD.index(k)
-        late = LATE[chip]
-        for r in (1 - late, late):
-            for s in range(S):
-                c = 2 * s + r
-                srcs = [T.la[c], T.lb[c]]
-                need = 8
-                if r == late:
-                    srcs.append(T.lp[s])
-                    need += 4
-                g.wait_ge(T.sem["in%d" % c], need)
-                g.remote_dma_fused(
-                    [RemoteDMATransfer(dst_ids=[_dst(topo, ROOT)], dma_engine_mask=0x00FF,
-                                       remote_sem=T.sem[("l%d" if r == late else "e%d") % s],
-                                       srcs=srcs, dsts=[(T.rlate if r == late else T.rearly)[4 * c + h]], alu_op=1)],
-                    local_sem=T.sem.sent)
+        mine = MINE[chip]
+        for s in range(S):
+            c = 2 * s + 1 - mine
+            g.wait_ge(T.sem["in%d" % c], 8)
+            g.remote_dma_fused(
+                [RemoteDMATransfer(dst_ids=[_dst(topo, (3 - chip) * 8 + k)], dma_engine_mask=0x00FF,
+                                   remote_sem=T.sem["in%d" % c],
+                                   srcs=[T.la[c], T.lb[c]], dsts=[T.lq[s]], alu_op=1)],
+                local_sem=T.sem.sent)
+        for s in range(S):
+            c = 2 * s + mine
+            g.wait_ge(T.sem["in%d" % c], 24)
+            g.remote_dma_fused(
+                [RemoteDMATransfer(dst_ids=[_dst(topo, ROOT)], dma_engine_mask=0x00FF,
+                                   remote_sem=T.sem["l%d" % s],
+                                   srcs=[T.la[c], T.lb[c], T.lp[s], T.lr[s], T.lq[s]],
+                                   dsts=[T.rsum[4 * c + h]], alu_op=1)],
+                local_sem=T.sem.sent)
         g.wait_ge(T.sem.sent, 16 * S)

from concourse.bass import DstId, RemoteDMATransfer

S = 2
BR = 128 // S
CR = BR // 2
N = CR * 2
FOLD = (2, 3, 6, 7)
ROOT = 20
MINE = {0: 1, 3: 0}
GATHER = (3, 0)

SCRATCH = {
    "st": ("dram", [8 * S, 128, N], "float32"),
    "la": ("dram", [2 * S, 128, N], "float32"),
    "lb": ("dram", [2 * S, 128, N], "float32"),
    "lp": ("dram", [S, 128, N], "float32"),
    "lr": ("dram", [S, 128, N], "float32"),
    "lq": ("dram", [S, 128, N], "float32"),
    "rsum": ("dram", [8 * S, 128, N], "float32"),
}
SEMAPHORES = ["sent", "fin"]
for _s in range(S):
    SEMAPHORES += ["ld%d" % (2 * _s), "ld%d" % (2 * _s + 1), "in%d" % (2 * _s), "in%d" % (2 * _s + 1), "l%d" % _s]


def _dst(topo, core):
    a = topo.addr(core)
    return DstId(rid=a[0], pnc=a[1])


def rank_program(g, core, T, topo):
    chip, k = core // 8, core % 8
    land = T.la if k == 0 else T.lb
    queues = (g.sync, g.scalar)

    if k in (0, 4) and chip in (1, 2):
        for s in range(S):
            queues[s % 2].dma_start(T.st[8 * s:8 * s + 8],
                                    T.x[BR * s:BR * s + BR, :]).then_inc(T.sem["ld%d" % s], 16)
        for s in range(S):
            g.wait_ge(T.sem["ld%d" % s], 16)
            g.remote_dma_fused(
                [RemoteDMATransfer(dst_ids=[_dst(topo, chip * 8 + FOLD[h])], dma_engine_mask=0x3 << (8 * r + 2 * h),
                                   remote_sem=T.sem["in%d" % s], src=T.st[8 * s + 4 * r + h],
                                   dst=land[2 * s + r]) for r in range(2) for h in range(4)],
                local_sem=T.sem.sent)
        if core == ROOT:
            for s in range(S):
                queues[s % 2].wait_ge(T.sem["l%d" % s], 64)
                queues[s % 2].dma_start(T.y[BR * s:BR * s + BR, :], T.rsum[8 * s:8 * s + 8]).then_inc(T.sem.fin, 16)
        g.wait_ge(T.sem.sent, 16 * S)
        if core == ROOT:
            g.wait_ge(T.sem.fin, 16 * S)
        return

    if k in (0, 4):
        mine = MINE[chip]
        order = [2 * s + (1 - mine) for s in range(S)] + [2 * s + mine for s in range(S)]
        for i, c in enumerate(order):
            queues[i % 2].dma_start(T.st[4 * c:4 * c + 4],
                                    T.x[CR * c:CR * c + CR, :]).then_inc(T.sem["ld%d" % c], 16)
        for c in order:
            g.wait_ge(T.sem["ld%d" % c], 16)
            g.remote_dma_fused(
                [RemoteDMATransfer(dst_ids=[_dst(topo, chip * 8 + FOLD[h])], dma_engine_mask=0xF << (4 * h),
                                   remote_sem=T.sem["in%d" % c], src=T.st[4 * c + h],
                                   dst=land[c]) for h in range(4)],
                local_sem=T.sem.sent)
        g.wait_ge(T.sem.sent, 32 * S)
        return

    if k in FOLD and chip in (1, 2):
        out = T.lp if chip == 1 else T.lr
        for s in range(S):
            g.wait_ge(T.sem["in%d" % s], 8)
            g.remote_dma_fused(
                [RemoteDMATransfer(dst_ids=[_dst(topo, GATHER[r] * 8 + k)], dma_engine_mask=0xF << (4 * r),
                                   remote_sem=T.sem["in%d" % (2 * s + r)],
                                   srcs=[T.la[2 * s + r], T.lb[2 * s + r]], dsts=[out[s]], alu_op=1)
                 for r in range(2)],
                local_sem=T.sem.sent)
        g.wait_ge(T.sem.sent, 8 * S)
        return

    if k in FOLD:
        h = FOLD.index(k)
        mine = MINE[chip]
        for s in range(S):
            c = 2 * s + 1 - mine
            g.wait_ge(T.sem["in%d" % c], 8)
            g.remote_dma_fused(
                [RemoteDMATransfer(dst_ids=[_dst(topo, (3 - chip) * 8 + k)], dma_engine_mask=0x00FF,
                                   remote_sem=T.sem["in%d" % c],
                                   srcs=[T.la[c], T.lb[c]], dsts=[T.lq[s]], alu_op=1)],
                local_sem=T.sem.sent)
        for s in range(S):
            c = 2 * s + mine
            g.wait_ge(T.sem["in%d" % c], 24)
            g.remote_dma_fused(
                [RemoteDMATransfer(dst_ids=[_dst(topo, ROOT)], dma_engine_mask=0x00FF,
                                   remote_sem=T.sem["l%d" % s],
                                   srcs=[T.la[c], T.lb[c], T.lp[s], T.lr[s], T.lq[s]],
                                   dsts=[T.rsum[4 * c + h]], alu_op=1)],
                local_sem=T.sem.sent)
        g.wait_ge(T.sem.sent, 16 * S)
